import numpy as np, ml_dtypes
CORES = [1,129,9,137,57,185,105,233,113,241,121,249]
N = 12
import mx_ref
NC = 256
BF = ml_dtypes.bfloat16
def setup_inputs(rng):
    def f(*shape):
        return mx_ref.flush((rng.standard_normal(shape, dtype=np.float32) * np.exp2(rng.integers(-2, 3, shape[:-1] + (1,)))).astype(BF))
    return {"w": f(N, 128, N * 512), "x": f(N, 128, 4 * NC)}
def setup_inputs_blocks(rng):
    d = setup_inputs(rng)
    for k in ("w", "x"): d[k] = mx_ref.spread(d[k], rng, 2)
    return d
def setup_inputs_wide(rng):
    d = setup_inputs(rng)
    for k in ("w", "x"): d[k] = mx_ref.flush((d[k].astype(np.float32) * np.exp2(rng.integers(-8, 9, (N, 1, 1))).astype(np.float32)).astype(BF))
    return d
def setup_inputs_zeros(rng):
    d = setup_inputs(rng); v = d["x"].reshape(N, 128, -1, 4).copy()
    v[np.broadcast_to((rng.random((N, 1, v.shape[2], 1)) < 0.33), v.shape)] = 0
    d["x"] = v.reshape(d["x"].shape)
    return d
def reference(w, x):
    QX = [mx_ref.quantize(x[j]) for j in range(N)]
    y = np.zeros((N, 128, NC), np.float32)
    for r in range(N):
        for j in range(N):
            p = mx_ref.matmul(mx_ref.quantize(w[r][:, 512 * j:512 * j + 512]), QX[j])
            y[r] = p if j == 0 else y[r] + p
    return {"y": y}

@@ -1,0 +1,244 @@
+from concourse.bass import DstId, RemoteDMATransfer
+from concourse.mybir import dt
+
+N = 12
+WORLD = 256
+NC = 256
+WC = 128
+WBLK = 4
+NBLK = N // WBLK
+EARLY = 1
+
+SCRATCH = {
+    "xb": ("sbuf", [128, 4 * NC], "bfloat16"),
+    "wb": ("sbuf", [128, 4 * WC * N], "bfloat16"),
+    "xq": ("sbuf", [128, NC * N], "float8_e4m3fn_x4"),
+    "xs": ("sbuf", [128, NC * N], "uint8"),
+    "wq": ("sbuf", [128, WC * N], "float8_e4m3fn_x4"),
+    "ws": ("sbuf", [128, WC * N], "uint8"),
+    "acc": ("psum", [128, 512], "float32"),
+    "yb": ("sbuf", [128, NC], "float32"),
+}
+SEMAPHORES = (["xl", "xd", "go", "mm", "cp", "st", "sent"]
+              + ["wl%d" % k for k in range(NBLK)] + ["wd%d" % k for k in range(NBLK)]
+              + ["c%d" % j for j in range(N)] + ["s%d" % j for j in range(N)])
+
+_CACHE = {}
+
+
+def _bits(m):
+    return bin(m).count("1")
+
+
+def lane_masks(core, sends, topo):
+    lo = hi = -1
+    for d, lane in sends:
+        if lane == 0:
+            lo &= topo.mask(core, d)
+        else:
+            hi &= topo.mask(core, d)
+    return (lo, hi & ~lo)
+
+
+def build_plan(cores, topo):
+    world = range(WORLD)
+    place = {}
+    for c in world:
+        place.setdefault((topo.host(c), topo.chip(c)), []).append(c)
+
+    def chip_of(c):
+        return place[(topo.host(c), topo.chip(c))]
+
+    def mate_chip_of(c):
+        return [d for d in world if topo.mates(c, d)]
+
+    def roles(ref, chip):
+        other = mate_chip_of(chip[0])[0]
+        out = {"np": [], "fp": [], "nn": [], "fn": []}
+        for c in chip:
+            if c in cores:
+                continue
+            k = ("n" if topo.die(c) == topo.die(ref) else "f") + ("p" if topo.may_write(c, other) else "n")
+            out[k].append(c)
+        return out
+
+    mate_rank = {}
+    for r, c in enumerate(cores):
+        for q, d in enumerate(cores):
+            if topo.mates(c, d):
+                mate_rank[r] = q
+    full = [r for r in range(len(cores)) if r in mate_rank]
+    half = [r for r in range(len(cores)) if r not in mate_rank]
+    pairs = []
+    for r in full:
+        if not any(r in p for p in pairs):
+            pairs.append((r, mate_rank[r]))
+    col = {r: k for k, p in enumerate(pairs) for r in p}
+    nf, nh = len(pairs), len(half)
+
+    tree = {}
+
+    def send(src, tile, dst, lane=0):
+        tree.setdefault((src, tile), []).append((dst, lane))
+
+    fan = {}
+    for s, S in enumerate(cores):
+        ro = roles(S, chip_of(S))
+        if s in full:
+            a = col[s]
+            b_, a_, c_, d_ = ro["np"][0], ro["nn"][0], ro["fn"][0], ro["fn"][1]
+            for o, snd in ((1, b_), (2, c_), (3, d_)):
+                d = [r for r in pairs[(a + o) % nf] if topo.same_plane(S, cores[r])][0]
+                rd = roles(S, chip_of(cores[d]))
+                relay = (rd["np"][1], rd["fp"][0], rd["fp"][1])[o - 1]
+                send(snd, s, relay)
+                send(relay, s, cores[mate_rank[d]], 0)
+                send(relay, s, cores[d], 1)
+            near, far = [a_, a_], [c_, d_]
+            for i, h in enumerate(half):
+                slot = (a + i) % nh
+                snd = near.pop(0) if slot < nh // 2 else far.pop(0)
+                if topo.same_plane(S, cores[h]):
+                    send(snd, s, cores[h])
+                else:
+                    rd = roles(S, mate_chip_of(cores[h]))
+                    relay = (rd["np"] + rd["fp"])[slot]
+                    send(snd, s, relay)
+                    send(relay, s, cores[h])
+            send(b_, s, cores[mate_rank[s]])
+            fan[s] = [b_, c_, d_, a_] if topo.same_plane(S, cores[half[0]]) else [a_, c_, d_, b_]
+        else:
+            i = half.index(s)
+            near, far, cross_n, cross_f = [], [], [], []
+            for r in full:
+                nearside = (col[r] + i) % nf < nf // 2
+                if topo.same_plane(S, cores[r]):
+                    (near if nearside else far).append(cores[r])
+                else:
+                    (cross_n if nearside else cross_f).append(cores[r])
+            for o in range(1, nh):
+                (far if o % 2 == 0 else near).append(cores[half[(i + o) % nh]])
+            fan[s] = []
+            for ports, cross, same in ((ro["np"], cross_n, near), (ro["fp"], cross_f, far)):
+                for k, p in enumerate(ports):
+                    for d in [cross[k]] + same[k::len(ports)]:
+                        send(p, s, d)
+                    fan[s].append(p)
+            fan[s].sort(key=lambda c: -len(tree[(c, s)]))
+        for c in fan[s]:
+            send(S, s, c)
+
+    jobs, count, est = {}, {}, {}
+    for s, S in enumerate(cores):
+        est[(S, s)] = 0.0
+        todo = [S]
+        while todo:
+            c = todo.pop(0)
+            sends = tree.get((c, s))
+            if not sends:
+                continue
+            masks = lane_masks(c, sends, topo)
+            jobs.setdefault(c, []).append((s, sends, c == S))
+            clock = [est[(c, s)] + 1.0, est[(c, s)] + 1.0]
+            for d, lane in sends:
+                count[(d, s)] = _bits(masks[lane])
+                clock[lane] += 8.0 / _bits(masks[lane])
+                est[(d, s)] = clock[lane]
+                todo.append(d)
+    order, blocks = {}, {}
+    for r, R in enumerate(cores):
+        first = sorted(range(NBLK), key=lambda k: min(est[(R, j)] for j in range(WBLK * k, WBLK * (k + 1))))
+        free = 2.0 + 0.5 * len(fan[r])
+        ready = {k: (0.0 if n < EARLY else free + 1.6 * (n - EARLY + 1)) for n, k in enumerate(first)}
+        order[r] = sorted(range(len(cores)), key=lambda j: (max(est[(R, j)], ready[j // WBLK]), j))
+        blocks[r] = first
+    return {"jobs": jobs, "count": count, "order": order, "blocks": blocks, "est": est}
+
+
+def rank_program(g, core, T, topo):
+    if "plan" not in _CACHE:
+        _CACHE["plan"] = build_plan(list(T.cores), topo)
+    plan = _CACHE["plan"]
+    rank = T.rank_of(core)
+    jobs = plan["jobs"].get(core, [])
+    if rank is None and not jobs:
+        return
+    sem = T.sem
+    sent = [0]
+
+    def codes(j):
+        return T.xq[:, NC * j:NC * (j + 1)].bitcast(dt.uint8)
+
+    def plane(j):
+        return T.xs[:, NC * j:NC * (j + 1)]
+
+    def call(view, arrive, groups):
+        trs = []
+        for m, dsts in groups:
+            ids = []
+            for d in dsts:
+                rid, pid = topo.addr(d, core)
+                ids.append(DstId(rid=rid, pnc=pid))
+            trs.append(RemoteDMATransfer(dst_ids=ids, dma_engine_mask=m, remote_sem=arrive,
+                                         srcs=[view], dsts=[view] * len(dsts)))
+            sent[0] += _bits(m)
+        g.remote_dma_fused(trs, local_sem=sem.sent)
+
+    def pass_on(tile, sends, fused):
+        masks = lane_masks(core, sends, topo)
+        lanes = [[d for d, l in sends if l == k] for k in (0, 1)]
+        whole = [(masks[k], lanes[k]) for k in (0, 1) if lanes[k]]
+        if rank is None:
+            g.wait_ge(sem["s%d" % tile], plan["count"][(core, tile)])
+        call(plane(tile), sem["s%d" % tile], whole)
+        if rank is None:
+            g.wait_ge(sem["c%d" % tile], plan["count"][(core, tile)])
+        if fused:
+            call(codes(tile), sem["c%d" % tile], whole)
+        else:
+            for k in range(max(len(l) for l in lanes)):
+                call(codes(tile), sem["c%d" % tile], [(masks[n], [lanes[n][k]]) for n in (0, 1) if k < len(lanes[n])])
+
+    if rank is None:
+        for tile, sends, fused in jobs:
+            pass_on(tile, sends, fused)
+        g.wait_ge(sem.sent, sent[0])
+        return
+
+    order, blocks = plan["order"][rank], plan["blocks"][rank]
+    g.sync.dma_start(T.xb[:], T.x[:]).then_inc(sem.xl, 16)
+    g.vector.wait_ge(sem.xl, 16)
+    g.vector.quantize_mx(T.xq[:, NC * rank:NC * (rank + 1)], plane(rank), T.xb[:]).then_inc(sem.xd, 1)
+    g.wait_ge(sem.xd, 1)
+    for tile, sends, fused in jobs:
+        pass_on(tile, sends, fused)
+    g.sem_inc(sem.go, 1)
+    for n, k in enumerate(blocks):
+        if n == EARLY:
+            g.sync.wait_ge(sem.go, 1)
+        a, b = 4 * WC * WBLK * k, 4 * WC * WBLK * (k + 1)
+        g.sync.dma_start(T.wb[:, a:b], T.w[:, a:b]).then_inc(sem["wl%d" % k], 16)
+    for k in blocks:
+        a, b = WC * WBLK * k, WC * WBLK * (k + 1)
+        g.vector.wait_ge(sem["wl%d" % k], 16)
+        g.vector.quantize_mx(T.wq[:, a:b], T.ws[:, a:b], T.wb[:, 4 * a:4 * b]).then_inc(sem["wd%d" % k], 1)
+    seen = []
+    for n, j in enumerate(order):
+        if j // WBLK not in seen:
+            seen.append(j // WBLK)
+            g.tensor.wait_ge(sem["wd%d" % (j // WBLK)], 1)
+        if j == rank:
+            g.tensor.wait_ge(sem.xd, 1)
+        else:
+            g.tensor.wait_ge(sem["s%d" % j], plan["count"][(core, j)])
+            g.tensor.wait_ge(sem["c%d" % j], plan["count"][(core, j)])
+        mm = g.tensor.matmul_mx(T.acc[:, 0:NC], T.wq[:, WC * j:WC * (j + 1)], T.ws[:, WC * j:WC * (j + 1)],
+                                T.xq[:, NC * j:NC * (j + 1)], plane(j), n == 0, n == N - 1)
+        if n == N - 1:
+            mm.then_inc(sem.mm, 1)
+    g.vector.wait_ge(sem.mm, 1)
+    g.vector.tensor_copy(T.yb[:], T.acc[:, 0:NC]).then_inc(sem.cp, 1)
+    g.sync.wait_ge(sem.cp, 1)
+    g.sync.dma_start(T.y[:], T.yb[:]).then_inc(sem.st, 16)
+    g.sync.wait_ge(sem.st, 16)
+    g.wait_ge(sem.sent, sent[0])

@@ -5,9 +5,11 @@ N = 12
 WORLD = 256
 NC = 256
 WC = 128
-WBLK = 4
+WBLK = 2
 NBLK = N // WBLK
-EARLY = 1
+EARLY = 2
+HOP = 2.5
+LO, HI, ALL = 0, 1, 2
 
 SCRATCH = {
     "xb": ("sbuf", [128, 4 * NC], "bfloat16"),
@@ -30,14 +32,13 @@ def _bits(m):
     return bin(m).count("1")
 
 
-def lane_masks(core, sends, topo):
-    lo = hi = -1
-    for d, lane in sends:
-        if lane == 0:
-            lo &= topo.mask(core, d)
-        else:
-            hi &= topo.mask(core, d)
-    return (lo, hi & ~lo)
+def lane_masks(core, phases, topo):
+    m = [-1, -1, -1]
+    for ph in phases:
+        for lane, dsts in ph:
+            for d in dsts:
+                m[lane] &= topo.mask(core, d)
+    return (m[LO], m[HI] & ~m[LO], m[ALL])
 
 
 def build_plan(cores, topo):
@@ -78,55 +79,56 @@ def build_plan(cores, topo):
 
     tree = {}
 
-    def send(src, tile, dst, lane=0):
-        tree.setdefault((src, tile), []).append((dst, lane))
+    def one_by_one(dsts):
+        return [[(LO, [d])] for d in dsts]
 
-    fan = {}
     for s, S in enumerate(cores):
         ro = roles(S, chip_of(S))
         if s in full:
             a = col[s]
-            b_, a_, c_, d_ = ro["np"][0], ro["nn"][0], ro["fn"][0], ro["fn"][1]
-            for o, snd in ((1, b_), (2, c_), (3, d_)):
+            entry = []
+            for o in (1, 2, 3):
                 d = [r for r in pairs[(a + o) % nf] if topo.same_plane(S, cores[r])][0]
                 rd = roles(S, chip_of(cores[d]))
                 relay = (rd["np"][1], rd["fp"][0], rd["fp"][1])[o - 1]
-                send(snd, s, relay)
-                send(relay, s, cores[mate_rank[d]], 0)
-                send(relay, s, cores[d], 1)
-            near, far = [a_, a_], [c_, d_]
+                entry.append(relay)
+                tree[(relay, s)] = [[(LO, [cores[mate_rank[d]]]), (HI, [cores[d]])]]
+            own_plane = topo.same_plane(S, cores[half[0]])
+            lone = []
             for i, h in enumerate(half):
-                slot = (a + i) % nh
-                snd = near.pop(0) if slot < nh // 2 else far.pop(0)
-                if topo.same_plane(S, cores[h]):
-                    send(snd, s, cores[h])
+                if own_plane:
+                    lone.append(cores[h])
                 else:
                     rd = roles(S, mate_chip_of(cores[h]))
-                    relay = (rd["np"] + rd["fp"])[slot]
-                    send(snd, s, relay)
-                    send(relay, s, cores[h])
-            send(b_, s, cores[mate_rank[s]])
-            fan[s] = [b_, c_, d_, a_] if topo.same_plane(S, cores[half[0]]) else [a_, c_, d_, b_]
+                    relay = (rd["np"] + rd["fp"])[(a + i) % nh]
+                    lone.append(relay)
+                    tree[(relay, s)] = [[(LO, [cores[h]])]]
+            lone = lone[a % nh:] + lone[:a % nh]
+            mate = cores[mate_rank[s]]
+            h1, h2, h3 = ro["fn"][0], ro["fn"][1], ro["np"][0]
+            if own_plane:
+                tree[(S, s)] = [[(LO, entry), (HI, [h1, h2, h3])]]
+                tree[(h1, s)] = one_by_one(lone[0:2])
+                tree[(h2, s)] = one_by_one(lone[2:4])
+                tree[(h3, s)] = one_by_one([mate])
+            else:
+                tree[(S, s)] = [[(ALL, [h1, h2, h3])], [(LO, entry)]]
+                tree[(h1, s)] = one_by_one(lone[0:2])
+                tree[(h2, s)] = one_by_one(lone[2:3])
+                tree[(h3, s)] = one_by_one([lone[3], mate])
         else:
             i = half.index(s)
-            near, far, cross_n, cross_f = [], [], [], []
-            for r in full:
-                nearside = (col[r] + i) % nf < nf // 2
-                if topo.same_plane(S, cores[r]):
-                    (near if nearside else far).append(cores[r])
-                else:
-                    (cross_n if nearside else cross_f).append(cores[r])
-            for o in range(1, nh):
-                (far if o % 2 == 0 else near).append(cores[half[(i + o) % nh]])
-            fan[s] = []
-            for ports, cross, same in ((ro["np"], cross_n, near), (ro["fp"], cross_f, far)):
-                for k, p in enumerate(ports):
-                    for d in [cross[k]] + same[k::len(ports)]:
-                        send(p, s, d)
-                    fan[s].append(p)
-            fan[s].sort(key=lambda c: -len(tree[(c, s)]))
-        for c in fan[s]:
-            send(S, s, c)
+            others = [cores[half[(i + o) % nh]] for o in range(1, nh)]
+            same = [cores[r] for r in full if topo.same_plane(S, cores[r])]
+            cross = [cores[r] for r in full if not topo.same_plane(S, cores[r])]
+            same = same[i:] + same[:i]
+            cross = cross[i:] + cross[:i]
+            h1, h2, h3, h4 = ro["fn"][0], ro["fp"][0], ro["fp"][1], ro["np"][0]
+            tree[(S, s)] = [[(LO, others + same[3:4]), (HI, [h1, h2, h3, h4])]]
+            tree[(h1, s)] = one_by_one(same[0:3])
+            tree[(h2, s)] = one_by_one(cross[0:2])
+            tree[(h3, s)] = one_by_one(cross[2:3])
+            tree[(h4, s)] = one_by_one(cross[3:4])
 
     jobs, count, est = {}, {}, {}
     for s, S in enumerate(cores):
@@ -134,22 +136,27 @@ def build_plan(cores, topo):
         todo = [S]
         while todo:
             c = todo.pop(0)
-            sends = tree.get((c, s))
-            if not sends:
+            phases = tree.get((c, s))
+            if not phases:
                 continue
-            masks = lane_masks(c, sends, topo)
-            jobs.setdefault(c, []).append((s, sends, c == S))
-            clock = [est[(c, s)] + 1.0, est[(c, s)] + 1.0]
-            for d, lane in sends:
-                count[(d, s)] = _bits(masks[lane])
-                clock[lane] += 8.0 / _bits(masks[lane])
-                est[(d, s)] = clock[lane]
-                todo.append(d)
+            masks = lane_masks(c, phases, topo)
+            jobs.setdefault(c, []).append((s, phases))
+            clock = [est[(c, s)] + HOP, est[(c, s)] + HOP]
+            for ph in phases:
+                for lane, dsts in ph:
+                    for d in dsts:
+                        count[(d, s)] = _bits(masks[lane])
+                        if lane == ALL:
+                            clock = [max(clock) + 8.0 / _bits(masks[lane])] * 2
+                            est[(d, s)] = clock[0]
+                        else:
+                            clock[lane] += 8.0 / _bits(masks[lane])
+                            est[(d, s)] = clock[lane]
+                        todo.append(d)
     order, blocks = {}, {}
     for r, R in enumerate(cores):
         first = sorted(range(NBLK), key=lambda k: min(est[(R, j)] for j in range(WBLK * k, WBLK * (k + 1))))
-        free = 2.0 + 0.5 * len(fan[r])
-        ready = {k: (0.0 if n < EARLY else free + 1.6 * (n - EARLY + 1)) for n, k in enumerate(first)}
+        ready = {k: (0.0 if n < EARLY else HOP + 4.0 + 0.8 * (n - EARLY + 1)) for n, k in enumerate(first)}
         order[r] = sorted(range(len(cores)), key=lambda j: (max(est[(R, j)], ready[j // WBLK]), j))
         blocks[r] = first
     return {"jobs": jobs, "count": count, "order": order, "blocks": blocks, "est": est}
@@ -184,24 +191,28 @@ def rank_program(g, core, T, topo):
             sent[0] += _bits(m)
         g.remote_dma_fused(trs, local_sem=sem.sent)
 
-    def pass_on(tile, sends, fused):
-        masks = lane_masks(core, sends, topo)
-        lanes = [[d for d, l in sends if l == k] for k in (0, 1)]
-        whole = [(masks[k], lanes[k]) for k in (0, 1) if lanes[k]]
+    def pass_on(tile, phases):
+        masks = lane_masks(core, phases, topo)
+        merged = []
+        for ph in phases:
+            key = [lane for lane, dsts in ph]
+            if merged and merged[-1][0] == key:
+                for k, (lane, dsts) in enumerate(ph):
+                    merged[-1][1][k][1].extend(dsts)
+            else:
+                merged.append((key, [(lane, list(dsts)) for lane, dsts in ph]))
         if rank is None:
             g.wait_ge(sem["s%d" % tile], plan["count"][(core, tile)])
-        call(plane(tile), sem["s%d" % tile], whole)
+        for key, ph in merged:
+            call(plane(tile), sem["s%d" % tile], [(masks[lane], dsts) for lane, dsts in ph])
         if rank is None:
             g.wait_ge(sem["c%d" % tile], plan["count"][(core, tile)])
-        if fused:
-            call(codes(tile), sem["c%d" % tile], whole)
-        else:
-            for k in range(max(len(l) for l in lanes)):
-                call(codes(tile), sem["c%d" % tile], [(masks[n], [lanes[n][k]]) for n in (0, 1) if k < len(lanes[n])])
+        for ph in phases:
+            call(codes(tile), sem["c%d" % tile], [(masks[lane], dsts) for lane, dsts in ph])
 
     if rank is None:
-        for tile, sends, fused in jobs:
-            pass_on(tile, sends, fused)
+        for tile, phases in jobs:
+            pass_on(tile, phases)
         g.wait_ge(sem.sent, sent[0])
         return
 
@@ -210,8 +221,8 @@ def rank_program(g, core, T, topo):
     g.vector.wait_ge(sem.xl, 16)
     g.vector.quantize_mx(T.xq[:, NC * rank:NC * (rank + 1)], plane(rank), T.xb[:]).then_inc(sem.xd, 1)
     g.wait_ge(sem.xd, 1)
-    for tile, sends, fused in jobs:
-        pass_on(tile, sends, fused)
+    for tile, phases in jobs:
+        pass_on(tile, phases)
     g.sem_inc(sem.go, 1)
     for n, k in enumerate(blocks):
         if n == EARLY:

from concourse.bass import DstId, RemoteDMATransfer
from concourse.mybir import dt

N = 12
WORLD = 256
NC = 256
WC = 128
WBLK = 2
NBLK = N // WBLK
EARLY = 2
HOP = 2.5
LO, HI, ALL = 0, 1, 2

SCRATCH = {
    "xb": ("sbuf", [128, 4 * NC], "bfloat16"),
    "wb": ("sbuf", [128, 4 * WC * N], "bfloat16"),
    "xq": ("sbuf", [128, NC * N], "float8_e4m3fn_x4"),
    "xs": ("sbuf", [128, NC * N], "uint8"),
    "wq": ("sbuf", [128, WC * N], "float8_e4m3fn_x4"),
    "ws": ("sbuf", [128, WC * N], "uint8"),
    "acc": ("psum", [128, 512], "float32"),
    "yb": ("sbuf", [128, NC], "float32"),
}
SEMAPHORES = (["xl", "xd", "go", "mm", "cp", "st", "sent"]
              + ["wl%d" % k for k in range(NBLK)] + ["wd%d" % k for k in range(NBLK)]
              + ["c%d" % j for j in range(N)] + ["s%d" % j for j in range(N)])

_CACHE = {}


def _bits(m):
    return bin(m).count("1")


def lane_masks(core, phases, topo):
    m = [-1, -1, -1]
    for ph in phases:
        for lane, dsts in ph:
            for d in dsts:
                m[lane] &= topo.mask(core, d)
    return (m[LO], m[HI] & ~m[LO], m[ALL])


def build_plan(cores, topo):
    world = range(WORLD)
    place = {}
    for c in world:
        place.setdefault((topo.host(c), topo.chip(c)), []).append(c)

    def chip_of(c):
        return place[(topo.host(c), topo.chip(c))]

    def mate_chip_of(c):
        return [d for d in world if topo.mates(c, d)]

    def roles(ref, chip):
        other = mate_chip_of(chip[0])[0]
        out = {"np": [], "fp": [], "nn": [], "fn": []}
        for c in chip:
            if c in cores:
                continue
            k = ("n" if topo.die(c) == topo.die(ref) else "f") + ("p" if topo.may_write(c, other) else "n")
            out[k].append(c)
        return out

    mate_rank = {}
    for r, c in enumerate(cores):
        for q, d in enumerate(cores):
            if topo.mates(c, d):
                mate_rank[r] = q
    full = [r for r in range(len(cores)) if r in mate_rank]
    half = [r for r in range(len(cores)) if r not in mate_rank]
    pairs = []
    for r in full:
        if not any(r in p for p in pairs):
            pairs.append((r, mate_rank[r]))
    col = {r: k for k, p in enumerate(pairs) for r in p}
    nf, nh = len(pairs), len(half)

    tree = {}

    def one_by_one(dsts):
        return [[(LO, [d])] for d in dsts]

    for s, S in enumerate(cores):
        ro = roles(S, chip_of(S))
        if s in full:
            a = col[s]
            entry = []
            for o in (1, 2, 3):
                d = [r for r in pairs[(a + o) % nf] if topo.same_plane(S, cores[r])][0]
                rd = roles(S, chip_of(cores[d]))
                relay = (rd["np"][1], rd["fp"][0], rd["fp"][1])[o - 1]
                entry.append(relay)
                tree[(relay, s)] = [[(LO, [cores[mate_rank[d]]]), (HI, [cores[d]])]]
            own_plane = topo.same_plane(S, cores[half[0]])
            lone = []
            for i, h in enumerate(half):
                if own_plane:
                    lone.append(cores[h])
                else:
                    rd = roles(S, mate_chip_of(cores[h]))
                    relay = (rd["np"] + rd["fp"])[(a + i) % nh]
                    lone.append(relay)
                    tree[(relay, s)] = [[(LO, [cores[h]])]]
            lone = lone[a % nh:] + lone[:a % nh]
            mate = cores[mate_rank[s]]
            h1, h2, h3 = ro["fn"][0], ro["fn"][1], ro["np"][0]
            if own_plane:
                tree[(S, s)] = [[(LO, entry), (HI, [h1, h2, h3])]]
                tree[(h1, s)] = one_by_one(lone[0:2])
                tree[(h2, s)] = one_by_one(lone[2:4])
                tree[(h3, s)] = one_by_one([mate])
            else:
                tree[(S, s)] = [[(ALL, [h1, h2, h3])], [(LO, entry)]]
                tree[(h1, s)] = one_by_one(lone[0:2])
                tree[(h2, s)] = one_by_one(lone[2:3])
                tree[(h3, s)] = one_by_one([lone[3], mate])
        else:
            i = half.index(s)
            others = [cores[half[(i + o) % nh]] for o in range(1, nh)]
            same = [cores[r] for r in full if topo.same_plane(S, cores[r])]
            cross = [cores[r] for r in full if not topo.same_plane(S, cores[r])]
            same = same[i:] + same[:i]
            cross = cross[i:] + cross[:i]
            h1, h2, h3, h4 = ro["fn"][0], ro["fp"][0], ro["fp"][1], ro["np"][0]
            tree[(S, s)] = [[(LO, others + same[3:4]), (HI, [h1, h2, h3, h4])]]
            tree[(h1, s)] = one_by_one(same[0:3])
            tree[(h2, s)] = one_by_one(cross[0:2])
            tree[(h3, s)] = one_by_one(cross[2:3])
            tree[(h4, s)] = one_by_one(cross[3:4])

    jobs, count, est = {}, {}, {}
    for s, S in enumerate(cores):
        est[(S, s)] = 0.0
        todo = [S]
        while todo:
            c = todo.pop(0)
            phases = tree.get((c, s))
            if not phases:
                continue
            masks = lane_masks(c, phases, topo)
            jobs.setdefault(c, []).append((s, phases))
            clock = [est[(c, s)] + HOP, est[(c, s)] + HOP]
            for ph in phases:
                for lane, dsts in ph:
                    for d in dsts:
                        count[(d, s)] = _bits(masks[lane])
                        if lane == ALL:
                            clock = [max(clock) + 8.0 / _bits(masks[lane])] * 2
                            est[(d, s)] = clock[0]
                        else:
                            clock[lane] += 8.0 / _bits(masks[lane])
                            est[(d, s)] = clock[lane]
                        todo.append(d)
    order, blocks = {}, {}
    for r, R in enumerate(cores):
        first = sorted(range(NBLK), key=lambda k: min(est[(R, j)] for j in range(WBLK * k, WBLK * (k + 1))))
        ready = {k: (0.0 if n < EARLY else HOP + 4.0 + 0.8 * (n - EARLY + 1)) for n, k in enumerate(first)}
        order[r] = sorted(range(len(cores)), key=lambda j: (max(est[(R, j)], ready[j // WBLK]), j))
        blocks[r] = first
    return {"jobs": jobs, "count": count, "order": order, "blocks": blocks, "est": est}


def rank_program(g, core, T, topo):
    if "plan" not in _CACHE:
        _CACHE["plan"] = build_plan(list(T.cores), topo)
    plan = _CACHE["plan"]
    rank = T.rank_of(core)
    jobs = plan["jobs"].get(core, [])
    if rank is None and not jobs:
        return
    sem = T.sem
    sent = [0]

    def codes(j):
        return T.xq[:, NC * j:NC * (j + 1)].bitcast(dt.uint8)

    def plane(j):
        return T.xs[:, NC * j:NC * (j + 1)]

    def call(view, arrive, groups):
        trs = []
        for m, dsts in groups:
            ids = []
            for d in dsts:
                rid, pid = topo.addr(d, core)
                ids.append(DstId(rid=rid, pnc=pid))
            trs.append(RemoteDMATransfer(dst_ids=ids, dma_engine_mask=m, remote_sem=arrive,
                                         srcs=[view], dsts=[view] * len(dsts)))
            sent[0] += _bits(m)
        g.remote_dma_fused(trs, local_sem=sem.sent)

    def pass_on(tile, phases):
        masks = lane_masks(core, phases, topo)
        merged = []
        for ph in phases:
            key = [lane for lane, dsts in ph]
            if merged and merged[-1][0] == key:
                for k, (lane, dsts) in enumerate(ph):
                    merged[-1][1][k][1].extend(dsts)
            else:
                merged.append((key, [(lane, list(dsts)) for lane, dsts in ph]))
        if rank is None:
            g.wait_ge(sem["s%d" % tile], plan["count"][(core, tile)])
        for key, ph in merged:
            call(plane(tile), sem["s%d" % tile], [(masks[lane], dsts) for lane, dsts in ph])
        if rank is None:
            g.wait_ge(sem["c%d" % tile], plan["count"][(core, tile)])
        for ph in phases:
            call(codes(tile), sem["c%d" % tile], [(masks[lane], dsts) for lane, dsts in ph])

    if rank is None:
        for tile, phases in jobs:
            pass_on(tile, phases)
        g.wait_ge(sem.sent, sent[0])
        return

    order, blocks = plan["order"][rank], plan["blocks"][rank]
    g.sync.dma_start(T.xb[:], T.x[:]).then_inc(sem.xl, 16)
    g.vector.wait_ge(sem.xl, 16)
    g.vector.quantize_mx(T.xq[:, NC * rank:NC * (rank + 1)], plane(rank), T.xb[:]).then_inc(sem.xd, 1)
    g.wait_ge(sem.xd, 1)
    for tile, phases in jobs:
        pass_on(tile, phases)
    g.sem_inc(sem.go, 1)
    for n, k in enumerate(blocks):
        if n == EARLY:
            g.sync.wait_ge(sem.go, 1)
        a, b = 4 * WC * WBLK * k, 4 * WC * WBLK * (k + 1)
        g.sync.dma_start(T.wb[:, a:b], T.w[:, a:b]).then_inc(sem["wl%d" % k], 16)
    for k in blocks:
        a, b = WC * WBLK * k, WC * WBLK * (k + 1)
        g.vector.wait_ge(sem["wl%d" % k], 16)
        g.vector.quantize_mx(T.wq[:, a:b], T.ws[:, a:b], T.wb[:, 4 * a:4 * b]).then_inc(sem["wd%d" % k], 1)
    seen = []
    for n, j in enumerate(order):
        if j // WBLK not in seen:
            seen.append(j // WBLK)
            g.tensor.wait_ge(sem["wd%d" % (j // WBLK)], 1)
        if j == rank:
            g.tensor.wait_ge(sem.xd, 1)
        else:
            g.tensor.wait_ge(sem["s%d" % j], plan["count"][(core, j)])
            g.tensor.wait_ge(sem["c%d" % j], plan["count"][(core, j)])
        mm = g.tensor.matmul_mx(T.acc[:, 0:NC], T.wq[:, WC * j:WC * (j + 1)], T.ws[:, WC * j:WC * (j + 1)],
                                T.xq[:, NC * j:NC * (j + 1)], plane(j), n == 0, n == N - 1)
        if n == N - 1:
            mm.then_inc(sem.mm, 1)
    g.vector.wait_ge(sem.mm, 1)
    g.vector.tensor_copy(T.yb[:], T.acc[:, 0:NC]).then_inc(sem.cp, 1)
    g.sync.wait_ge(sem.cp, 1)
    g.sync.dma_start(T.y[:], T.yb[:]).then_inc(sem.st, 16)
    g.sync.wait_ge(sem.st, 16)
    g.wait_ge(sem.sent, sent[0])
